import numpy as np, ml_dtypes
CORES = [113,118,241,246]
N = 4
F = 128
GROUPS = [[0,2],[1,3]]
def setup_inputs(rng):
    return {"x": rng.standard_normal((N, 128, F), dtype=np.float32).astype(ml_dtypes.bfloat16), "w": (rng.standard_normal((N, 128, 128), dtype=np.float32) / 11).astype(ml_dtypes.bfloat16)}
def setup_inputs_big(rng):
    d = setup_inputs(rng)
    for k in ("x", "w"): d[k] = (d[k].astype(np.float32) * 1024.0).astype(d[k].dtype)
    return d
def setup_inputs_small(rng):
    d = setup_inputs(rng)
    for k in ("x", "w"): d[k] = (d[k].astype(np.float32) * (1 / 1024.0)).astype(d[k].dtype)
    return d
def setup_inputs_apart(rng):
    d = setup_inputs(rng)
    f = (10.0 ** rng.permutation(np.linspace(-1.5, 1.5, N))).astype(np.float32).reshape(N, 1, 1)
    for k in ("x", "w"): d[k] = (d[k].astype(np.float32) * f).astype(d[k].dtype)
    return d
def reference(x, w):
    X, W = x.astype(np.float64), w.astype(np.float64)
    s = sum(W[g[0]].T @ np.maximum(sum(X[j] for j in g), 0.0) for g in GROUPS).astype(ml_dtypes.bfloat16)
    return {"y": np.broadcast_to(s, (N,) + s.shape)}

@@ -1,0 +1,117 @@
+from concourse.bass import DstId, RemoteDMATransfer
+from concourse.mybir import AluOpType
+
+F = 128
+
+SCRATCH = {
+    "first": ("sbuf", [128, 4 * F], "bfloat16"),
+    "second": ("sbuf", [128, 2 * F], "bfloat16"),
+    "zero": ("sbuf", [128, F], "bfloat16"),
+    "m": ("sbuf", [128, 2 * F], "bfloat16"),
+    "yb": ("sbuf", [128, F], "bfloat16"),
+    "neg": ("psum", [128, 512], "float32"),
+    "acc": ("psum", [128, 512], "float32"),
+}
+SEMAPHORES = ["loaded", "near", "far", "sent", "vz", "vn", "vm", "mm", "vy", "stored"]
+
+
+def _bits(mask):
+    return sum((mask >> k) & 1 for k in range(16))
+
+
+def rank_program(g, core, T, topo):
+    rank = T.rank_of(core)
+    if rank is None:
+        return
+    groups = T.tables["GROUPS"]
+    S = T.sem
+    gi = [k for k, grp in enumerate(groups) if rank in grp][0]
+    pos = groups[gi].index(rank)
+    og = 1 - gi
+
+    def same_chip(a, b):
+        return topo.host(a) == topo.host(b) and topo.chip(a) == topo.chip(b)
+
+    def plan(src):
+        far = [c for c in T.cores if c != src and not same_chip(c, src)]
+        near = [c for c in T.cores if c != src and same_chip(c, src)]
+        fm = topo.mask(src, far[0])
+        for c in far:
+            fm &= topo.mask(src, c)
+        nm = topo.mask(src, near[0])
+        for c in near:
+            nm &= topo.mask(src, c)
+        return far, fm, near, nm & ~fm
+
+    far, far_mask, near, near_mask = plan(core)
+    assert all(same_chip(T.cores[grp[pos]], core) and not same_chip(T.cores[grp[1 - pos]], core) for grp in groups)
+    n_far = sum(_bits(plan(c)[1]) for c in far)
+    n_near = sum(_bits(plan(c)[3]) for c in near)
+
+    def xf(k):
+        return T.first[:, (1 + k) * F:(2 + k) * F]
+
+    def wf(k):
+        return T.first[:, 3 * k * F:(3 * k + 1) * F]
+
+    def xs(k):
+        return T.second[:, k * F:(k + 1) * F]
+
+    near_x = xf if pos == 0 else xs
+    far_all = T.second[:, :] if pos == 0 else T.first[:, F:3 * F]
+    piece = T.first[:, 2 * gi * F:(2 * gi + 2) * F] if pos == 0 else xs(gi)
+
+    g.sync.dma_start(near_x(gi), T.x[:, :]).then_inc(S.loaded, 16)
+    n_load = 16
+    if pos == 0:
+        g.scalar.dma_start(wf(gi), T.w[:, :]).then_inc(S.loaded, 16)
+        n_load = 32
+
+    g.wait_ge(S.loaded, n_load)
+    ids = []
+    for c in far:
+        rid, pid = topo.addr(c, core)
+        ids.append(DstId(rid=rid, pnc=pid))
+    g.remote_dma_fused(
+        [RemoteDMATransfer(dst_ids=ids, dma_engine_mask=far_mask, remote_sem=S.far,
+                           srcs=[piece], dsts=[piece for _ in far], alu_op=0)],
+        local_sem=S.sent)
+    n_sent = _bits(far_mask)
+    for c in near:
+        rid, pid = topo.addr(c, core)
+        g.remote_dma(piece, piece, S.near, S.sent, pid, rid, near_mask)
+        n_sent += _bits(near_mask)
+
+    v = g.vector
+    v.memset(T.zero[:, :], 0.0).then_inc(S.vz, 1)
+    v.wait_ge(S.vz, 1)
+    v.wait_ge(S.loaded, n_load)
+    v.tensor_tensor(T.neg[:, gi * F:(gi + 1) * F], T.zero[:, :], near_x(gi), AluOpType.subtract).then_inc(S.vn, 1)
+    v.wait_ge(S.near, n_near)
+    v.tensor_tensor(T.neg[:, og * F:(og + 1) * F], T.zero[:, :], near_x(og), AluOpType.subtract).then_inc(S.vn, 1)
+    v.wait_ge(S.vn, 2)
+    v.wait_ge(S.far, n_far)
+    v.tensor_tensor(T.m[:, :], far_all, T.neg[:, 0:2 * F], AluOpType.max).then_inc(S.vm, 1)
+
+    t = g.tensor
+    t.wait_ge(S.loaded, n_load)
+    if pos == 0:
+        t.matmul(T.acc[:, 0:F], wf(gi), near_x(gi), True, False)
+        t.wait_ge(S.near, n_near)
+        t.matmul(T.acc[:, 0:F], wf(og), near_x(og), False, False)
+    else:
+        t.wait_ge(S.near, n_near)
+        t.wait_ge(S.far, n_far)
+        t.matmul(T.acc[:, 0:F], wf(gi), near_x(gi), True, False)
+        t.matmul(T.acc[:, 0:F], wf(og), near_x(og), False, False)
+    t.wait_ge(S.vm, 1)
+    t.matmul(T.acc[:, 0:F], wf(0), T.m[:, 0:F], False, False)
+    t.matmul(T.acc[:, 0:F], wf(1), T.m[:, F:2 * F], False, True).then_inc(S.mm, 1)
+
+    v.wait_ge(S.mm, 1)
+    v.tensor_copy(T.yb[:, :], T.acc[:, 0:F]).then_inc(S.vy, 1)
+
+    g.sync.wait_ge(S.vy, 1)
+    g.sync.dma_start(T.y[:, :], T.yb[:, :]).then_inc(S.stored, 16)
+    g.sync.wait_ge(S.stored, 16)
+    g.wait_ge(S.sent, n_sent)

@@ -12,7 +12,8 @@ SCRATCH = {
     "neg": ("psum", [128, 512], "float32"),
     "acc": ("psum", [128, 512], "float32"),
 }
-SEMAPHORES = ["loaded", "near", "far", "sent", "vz", "vn", "vm", "mm", "vy", "stored"]
+SEMAPHORES = ["lx", "lw", "go", "near", "fa", "fb", "fw", "sent",
+              "vz", "vn", "vs", "v1", "v2", "mm", "vy", "stored"]
 
 
 def _bits(mask):
@@ -32,21 +33,26 @@ def rank_program(g, core, T, topo):
     def same_chip(a, b):
         return topo.host(a) == topo.host(b) and topo.chip(a) == topo.chip(b)
 
-    def plan(src):
-        far = [c for c in T.cores if c != src and not same_chip(c, src)]
-        near = [c for c in T.cores if c != src and same_chip(c, src)]
-        fm = topo.mask(src, far[0])
-        for c in far:
-            fm &= topo.mask(src, c)
-        nm = topo.mask(src, near[0])
-        for c in near:
-            nm &= topo.mask(src, c)
-        return far, fm, near, nm & ~fm
+    def masks(src):
+        fm = nm = None
+        for c in T.cores:
+            if c == src:
+                continue
+            k = topo.mask(src, c)
+            if same_chip(c, src):
+                nm = k if nm is None else nm & k
+            else:
+                fm = k if fm is None else fm & k
+        return fm, nm & ~fm
 
-    far, far_mask, near, near_mask = plan(core)
     assert all(same_chip(T.cores[grp[pos]], core) and not same_chip(T.cores[grp[1 - pos]], core) for grp in groups)
-    n_far = sum(_bits(plan(c)[1]) for c in far)
-    n_near = sum(_bits(plan(c)[3]) for c in near)
+    far_mask, near_mask = masks(core)
+    partner = T.cores[groups[gi][1 - pos]]
+    other = T.cores[groups[og][1 - pos]]
+    mate = T.cores[groups[og][pos]]
+    n_fa = _bits(masks(partner)[0])
+    n_fb = _bits(masks(other)[0])
+    n_near = _bits(masks(mate)[1])
 
     def xf(k):
         return T.first[:, (1 + k) * F:(2 + k) * F]
@@ -57,61 +63,89 @@ def rank_program(g, core, T, topo):
     def xs(k):
         return T.second[:, k * F:(k + 1) * F]
 
-    near_x = xf if pos == 0 else xs
-    far_all = T.second[:, :] if pos == 0 else T.first[:, F:3 * F]
-    piece = T.first[:, 2 * gi * F:(2 * gi + 2) * F] if pos == 0 else xs(gi)
+    def mcol(k):
+        return T.m[:, k * F:(k + 1) * F]
 
-    g.sync.dma_start(near_x(gi), T.x[:, :]).then_inc(S.loaded, 16)
-    n_load = 16
-    if pos == 0:
-        g.scalar.dma_start(wf(gi), T.w[:, :]).then_inc(S.loaded, 16)
-        n_load = 32
+    n_sent = [0]
 
-    g.wait_ge(S.loaded, n_load)
-    ids = []
-    for c in far:
-        rid, pid = topo.addr(c, core)
-        ids.append(DstId(rid=rid, pnc=pid))
-    g.remote_dma_fused(
-        [RemoteDMATransfer(dst_ids=ids, dma_engine_mask=far_mask, remote_sem=S.far,
-                           srcs=[piece], dsts=[piece for _ in far], alu_op=0)],
-        local_sem=S.sent)
-    n_sent = _bits(far_mask)
-    for c in near:
-        rid, pid = topo.addr(c, core)
-        g.remote_dma(piece, piece, S.near, S.sent, pid, rid, near_mask)
-        n_sent += _bits(near_mask)
+    def send(ap, dst, sem, mask):
+        rid, pid = topo.addr(dst, core)
+        g.remote_dma(ap, ap, sem, S.sent, pid, rid, mask)
+        n_sent[0] += _bits(mask)
 
+    own_x = xf(gi) if pos == 0 else xs(gi)
+    neg0 = T.neg[:, 0:F]
+    neg1 = T.neg[:, F:2 * F]
+    acc = T.acc[:, 0:F]
     v = g.vector
+    t = g.tensor
+
+    g.sync.dma_start(own_x, T.x[:, :]).then_inc(S.lx, 16)
+    if pos == 0:
+        g.sync.sem_inc(S.go, 1)
+        g.scalar.wait_ge(S.go, 1)
+        g.scalar.dma_start(wf(gi), T.w[:, :]).then_inc(S.lw, 16)
+
     v.memset(T.zero[:, :], 0.0).then_inc(S.vz, 1)
     v.wait_ge(S.vz, 1)
-    v.wait_ge(S.loaded, n_load)
-    v.tensor_tensor(T.neg[:, gi * F:(gi + 1) * F], T.zero[:, :], near_x(gi), AluOpType.subtract).then_inc(S.vn, 1)
-    v.wait_ge(S.near, n_near)
-    v.tensor_tensor(T.neg[:, og * F:(og + 1) * F], T.zero[:, :], near_x(og), AluOpType.subtract).then_inc(S.vn, 1)
-    v.wait_ge(S.vn, 2)
-    v.wait_ge(S.far, n_far)
-    v.tensor_tensor(T.m[:, :], far_all, T.neg[:, 0:2 * F], AluOpType.max).then_inc(S.vm, 1)
+    v.wait_ge(S.lx, 16)
+    v.tensor_tensor(neg0, T.zero[:, :], own_x, AluOpType.subtract).then_inc(S.vn, 1)
 
-    t = g.tensor
-    t.wait_ge(S.loaded, n_load)
+    g.wait_ge(S.lx, 16)
     if pos == 0:
-        t.matmul(T.acc[:, 0:F], wf(gi), near_x(gi), True, False)
+        piece = T.first[:, 2 * gi * F:(2 * gi + 2) * F]
+        send(xf(gi), other, S.fb, far_mask)
+        g.wait_ge(S.lw, 16)
+        send(piece, partner, S.fa, far_mask)
+        send(wf(gi), other, S.fw, far_mask)
+        send(piece, mate, S.near, near_mask)
+
+        v.wait_ge(S.vn, 1)
+        v.wait_ge(S.fa, n_fa)
+        v.tensor_tensor(mcol(gi), xs(gi), neg0, AluOpType.max).then_inc(S.v1, 1)
+        v.wait_ge(S.fb, n_fb)
+        v.tensor_tensor(neg1, T.zero[:, :], xs(og), AluOpType.subtract).then_inc(S.vs, 1)
+        v.wait_ge(S.vs, 1)
+        v.wait_ge(S.near, n_near)
+        v.tensor_tensor(mcol(og), xf(og), neg1, AluOpType.max).then_inc(S.v2, 1)
+
+        t.wait_ge(S.lx, 16)
+        t.wait_ge(S.lw, 16)
+        t.matmul(acc, wf(gi), xf(gi), True, False)
+        t.wait_ge(S.v1, 1)
+        t.matmul(acc, wf(gi), mcol(gi), False, False)
+        t.wait_ge(S.fb, n_fb)
         t.wait_ge(S.near, n_near)
-        t.matmul(T.acc[:, 0:F], wf(og), near_x(og), False, False)
+        t.matmul(acc, wf(og), xs(og), False, False)
+        t.wait_ge(S.v2, 1)
+        t.matmul(acc, wf(og), mcol(og), False, True).then_inc(S.mm, 1)
     else:
-        t.wait_ge(S.near, n_near)
-        t.wait_ge(S.far, n_far)
-        t.matmul(T.acc[:, 0:F], wf(gi), near_x(gi), True, False)
-        t.matmul(T.acc[:, 0:F], wf(og), near_x(og), False, False)
-    t.wait_ge(S.vm, 1)
-    t.matmul(T.acc[:, 0:F], wf(0), T.m[:, 0:F], False, False)
-    t.matmul(T.acc[:, 0:F], wf(1), T.m[:, F:2 * F], False, True).then_inc(S.mm, 1)
+        send(xs(gi), partner, S.fa, far_mask)
+        send(xs(gi), other, S.fb, far_mask)
+        send(xs(gi), mate, S.near, near_mask)
+
+        v.wait_ge(S.near, n_near)
+        v.wait_ge(S.fb, n_fb)
+        v.tensor_tensor(neg1, xf(og), xs(og), AluOpType.add).then_inc(S.vs, 1)
+        v.wait_ge(S.vs, 1)
+        v.tensor_scalar(mcol(og), neg1, 0.0, None, AluOpType.max).then_inc(S.v2, 1)
+        v.wait_ge(S.vn, 1)
+        v.wait_ge(S.fa, n_fa)
+        v.tensor_tensor(mcol(gi), xf(gi), neg0, AluOpType.max).then_inc(S.v1, 1)
+
+        t.wait_ge(S.lx, 16)
+        t.wait_ge(S.fa, n_fa)
+        t.matmul(acc, wf(gi), xs(gi), True, False)
+        t.wait_ge(S.v1, 1)
+        t.matmul(acc, wf(gi), mcol(gi), False, False)
+        t.wait_ge(S.v2, 1)
+        t.wait_ge(S.fw, n_fb)
+        t.matmul(acc, wf(og), mcol(og), False, True).then_inc(S.mm, 1)
 
     v.wait_ge(S.mm, 1)
-    v.tensor_copy(T.yb[:, :], T.acc[:, 0:F]).then_inc(S.vy, 1)
+    v.tensor_copy(T.yb[:, :], acc).then_inc(S.vy, 1)
 
     g.sync.wait_ge(S.vy, 1)
     g.sync.dma_start(T.y[:, :], T.yb[:, :]).then_inc(S.stored, 16)
     g.sync.wait_ge(S.stored, 16)
-    g.wait_ge(S.sent, n_sent)
+    g.wait_ge(S.sent, n_sent[0])

from concourse.bass import DstId, RemoteDMATransfer
from concourse.mybir import AluOpType

F = 128

SCRATCH = {
    "first": ("sbuf", [128, 4 * F], "bfloat16"),
    "second": ("sbuf", [128, 2 * F], "bfloat16"),
    "zero": ("sbuf", [128, F], "bfloat16"),
    "m": ("sbuf", [128, 2 * F], "bfloat16"),
    "yb": ("sbuf", [128, F], "bfloat16"),
    "neg": ("psum", [128, 512], "float32"),
    "acc": ("psum", [128, 512], "float32"),
}
SEMAPHORES = ["lx", "lw", "go", "near", "fa", "fb", "fw", "sent",
              "vz", "vn", "vs", "v1", "v2", "mm", "vy", "stored"]


def _bits(mask):
    return sum((mask >> k) & 1 for k in range(16))


def rank_program(g, core, T, topo):
    rank = T.rank_of(core)
    if rank is None:
        return
    groups = T.tables["GROUPS"]
    S = T.sem
    gi = [k for k, grp in enumerate(groups) if rank in grp][0]
    pos = groups[gi].index(rank)
    og = 1 - gi

    def same_chip(a, b):
        return topo.host(a) == topo.host(b) and topo.chip(a) == topo.chip(b)

    def masks(src):
        fm = nm = None
        for c in T.cores:
            if c == src:
                continue
            k = topo.mask(src, c)
            if same_chip(c, src):
                nm = k if nm is None else nm & k
            else:
                fm = k if fm is None else fm & k
        return fm, nm & ~fm

    assert all(same_chip(T.cores[grp[pos]], core) and not same_chip(T.cores[grp[1 - pos]], core) for grp in groups)
    far_mask, near_mask = masks(core)
    partner = T.cores[groups[gi][1 - pos]]
    other = T.cores[groups[og][1 - pos]]
    mate = T.cores[groups[og][pos]]
    n_fa = _bits(masks(partner)[0])
    n_fb = _bits(masks(other)[0])
    n_near = _bits(masks(mate)[1])

    def xf(k):
        return T.first[:, (1 + k) * F:(2 + k) * F]

    def wf(k):
        return T.first[:, 3 * k * F:(3 * k + 1) * F]

    def xs(k):
        return T.second[:, k * F:(k + 1) * F]

    def mcol(k):
        return T.m[:, k * F:(k + 1) * F]

    n_sent = [0]

    def send(ap, dst, sem, mask):
        rid, pid = topo.addr(dst, core)
        g.remote_dma(ap, ap, sem, S.sent, pid, rid, mask)
        n_sent[0] += _bits(mask)

    own_x = xf(gi) if pos == 0 else xs(gi)
    neg0 = T.neg[:, 0:F]
    neg1 = T.neg[:, F:2 * F]
    acc = T.acc[:, 0:F]
    v = g.vector
    t = g.tensor

    g.sync.dma_start(own_x, T.x[:, :]).then_inc(S.lx, 16)
    if pos == 0:
        g.sync.sem_inc(S.go, 1)
        g.scalar.wait_ge(S.go, 1)
        g.scalar.dma_start(wf(gi), T.w[:, :]).then_inc(S.lw, 16)

    v.memset(T.zero[:, :], 0.0).then_inc(S.vz, 1)
    v.wait_ge(S.vz, 1)
    v.wait_ge(S.lx, 16)
    v.tensor_tensor(neg0, T.zero[:, :], own_x, AluOpType.subtract).then_inc(S.vn, 1)

    g.wait_ge(S.lx, 16)
    if pos == 0:
        piece = T.first[:, 2 * gi * F:(2 * gi + 2) * F]
        send(xf(gi), other, S.fb, far_mask)
        g.wait_ge(S.lw, 16)
        send(piece, partner, S.fa, far_mask)
        send(wf(gi), other, S.fw, far_mask)
        send(piece, mate, S.near, near_mask)

        v.wait_ge(S.vn, 1)
        v.wait_ge(S.fa, n_fa)
        v.tensor_tensor(mcol(gi), xs(gi), neg0, AluOpType.max).then_inc(S.v1, 1)
        v.wait_ge(S.fb, n_fb)
        v.tensor_tensor(neg1, T.zero[:, :], xs(og), AluOpType.subtract).then_inc(S.vs, 1)
        v.wait_ge(S.vs, 1)
        v.wait_ge(S.near, n_near)
        v.tensor_tensor(mcol(og), xf(og), neg1, AluOpType.max).then_inc(S.v2, 1)

        t.wait_ge(S.lx, 16)
        t.wait_ge(S.lw, 16)
        t.matmul(acc, wf(gi), xf(gi), True, False)
        t.wait_ge(S.v1, 1)
        t.matmul(acc, wf(gi), mcol(gi), False, False)
        t.wait_ge(S.fb, n_fb)
        t.wait_ge(S.near, n_near)
        t.matmul(acc, wf(og), xs(og), False, False)
        t.wait_ge(S.v2, 1)
        t.matmul(acc, wf(og), mcol(og), False, True).then_inc(S.mm, 1)
    else:
        send(xs(gi), partner, S.fa, far_mask)
        send(xs(gi), other, S.fb, far_mask)
        send(xs(gi), mate, S.near, near_mask)

        v.wait_ge(S.near, n_near)
        v.wait_ge(S.fb, n_fb)
        v.tensor_tensor(neg1, xf(og), xs(og), AluOpType.add).then_inc(S.vs, 1)
        v.wait_ge(S.vs, 1)
        v.tensor_scalar(mcol(og), neg1, 0.0, None, AluOpType.max).then_inc(S.v2, 1)
        v.wait_ge(S.vn, 1)
        v.wait_ge(S.fa, n_fa)
        v.tensor_tensor(mcol(gi), xf(gi), neg0, AluOpType.max).then_inc(S.v1, 1)

        t.wait_ge(S.lx, 16)
        t.wait_ge(S.fa, n_fa)
        t.matmul(acc, wf(gi), xs(gi), True, False)
        t.wait_ge(S.v1, 1)
        t.matmul(acc, wf(gi), mcol(gi), False, False)
        t.wait_ge(S.v2, 1)
        t.wait_ge(S.fw, n_fb)
        t.matmul(acc, wf(og), mcol(og), False, True).then_inc(S.mm, 1)

    v.wait_ge(S.mm, 1)
    v.tensor_copy(T.yb[:, :], acc).then_inc(S.vy, 1)

    g.sync.wait_ge(S.vy, 1)
    g.sync.dma_start(T.y[:, :], T.yb[:, :]).then_inc(S.stored, 16)
    g.sync.wait_ge(S.stored, 16)
    g.wait_ge(S.sent, n_sent[0])
